import numpy as np
import ml_dtypes


def mxq(x, axis, fmt="e4m3"):
    dtype, down = {"e4m3": (ml_dtypes.float8_e4m3fn, 7), "e5m2": (ml_dtypes.float8_e5m2, 14)}[fmt]
    v = np.moveaxis(np.asarray(x, np.float32).astype(ml_dtypes.bfloat16).astype(np.float64), axis, -1)
    blocks = v.reshape(v.shape[:-1] + (-1, 32))
    amax = np.abs(blocks).max(-1, keepdims=True)
    byte = np.maximum(np.where(amax > 0, np.frexp(amax)[1] - 1 + 127, 0) - down, 1)
    scale = np.exp2(byte - 127.0)
    codes = (blocks / scale).astype(np.float32).astype(dtype).astype(np.float64)
    return np.moveaxis((codes * scale).reshape(v.shape), -1, axis)


WIDE = False


def mx_kscale(k):
    if not WIDE:
        return np.ones(k)
    levels = np.array([10, -10, 5, -5, 0])
    if k % 512:
        return np.exp2(np.random.permutation(np.resize(levels, k // 32))).repeat(32)
    a = np.empty((k // 512, 16))
    for p in range(k // 512):
        a[p, :8] = np.random.permutation(np.resize(levels, 8))
        for g in range(8):
            far = levels[np.abs(levels - a[p, g]) >= 10]
            a[p, g + 8] = far[np.random.randint(len(far))]
    return np.exp2(a.ravel()).repeat(32)


def f64(x):
    return np.asarray(x).astype(np.float64)


def striped(idx):
    return np.tile(idx.reshape(-1, 16).T, (8, 1)).astype(np.uint16)


def unstriped(offs):
    return offs[:16].T.reshape(-1).astype(np.int64)


def pack_weight(w):
    k, n = w.shape
    w = f64(np.asarray(w, np.float32).astype(ml_dtypes.bfloat16)).reshape(k // 32, 32, n)
    amax = np.abs(w).max(1)
    byte = np.clip(np.where(amax > 0, np.frexp(amax)[1] - 1 + 127 - 7, 1), 1, 254)
    scaled = (w * np.exp2(127.0 - byte)[:, None, :]).reshape(k, n).astype(np.float32)
    words = np.ascontiguousarray(scaled.reshape(k // 512, 128, 4, n).transpose(0, 1, 3, 2)).astype(ml_dtypes.float8_e4m3fn).view(np.uint8)
    return words, np.ascontiguousarray(byte.astype(np.uint8).reshape(k // 512, 16, n))


def unpack_weight(words, scales):
    g, p, n, _ = words.shape
    vals = np.ascontiguousarray(words).view(ml_dtypes.float8_e4m3fn).astype(np.float64) * np.repeat(np.exp2(scales.astype(np.float64) - 127.0), 8, axis=1)[..., None]
    return vals.transpose(0, 1, 3, 2).reshape(g * 512, n)


def planes(y):
    n, m = y.shape
    v = y.astype(np.float32).astype(ml_dtypes.bfloat16).astype(np.float64).reshape(n // 32, 32, m)
    top = np.abs(v).max(1)
    byte = np.clip(np.where(top > 0, np.frexp(top)[1] - 1 + 127 - 7, 1), 1, 254)
    codes = (v * np.exp2(127.0 - byte)[:, None, :]).reshape(n, m).astype(np.float32).astype(ml_dtypes.float8_e4m3fn).view(np.uint8)
    words = codes.reshape(n // 512, 128, 4, m).transpose(0, 1, 3, 2)
    return np.ascontiguousarray(words), np.ascontiguousarray(byte.astype(np.uint8).reshape(n // 512, 16, m))


K, T, S, H, N, D = 512, 1024, 512, 512, 512, 8


def setup_inputs():
    n = np.random.standard_normal
    s = mx_kscale(K)[:, None]
    u = mx_kscale(H)
    packed_xT = pack_weight(n((K, T)) * s)
    return {
        "x_words": packed_xT[0],
        "x_scales": packed_xT[1],
        "w1": (n((K, N)) / np.sqrt(K) / s).astype(np.float32),
        "w2": (n((H, N)) / np.sqrt(H) / u[:, None]).astype(np.float32),
        "gam": (np.random.uniform(0.5, 1.5, (H, 1)) * u[:, None]).astype(np.float32),
        "offs": striped(np.random.permutation(T)[:S]),
    }


def reference(x_words, x_scales, w1, w2, gam, offs):
    xq = unpack_weight(x_words, x_scales)[:, unstriped(offs)]
    y = mxq(f64(w1), 0, "e4m3").T @ xq
    my = y.reshape(len(y), -1, D).mean(axis=2)
    dd = y - np.repeat(my, D, axis=1)
    ee = (dd) ** 2
    ss = np.sqrt(ee.reshape(len(ee), -1, D).mean(axis=2) + 0.1)
    z = f64(gam) * (dd / np.repeat(ss, D, axis=1))
    out_0 = mxq(f64(w2), 0, "e4m3").T @ mxq(z, 0, "e4m3")
    return (out_0,) + planes(out_0)

@@ -1,0 +1,259 @@
+from contextlib import ExitStack
+
+import concourse.mybir as mybir
+from concourse.masks import make_identity
+
+K, T, S, H, N, D = 512, 1024, 512, 512, 512, 8
+FLOPS = 2 * K * H * S + 2 * H * N * S
+
+F32 = mybir.dt.float32
+BF16 = mybir.dt.bfloat16
+I32 = mybir.dt.int32
+U32 = mybir.dt.uint32
+U16 = mybir.dt.uint16
+U8 = mybir.dt.uint8
+FP8X4 = mybir.dt.float8_e4m3fn_x4
+ALU = mybir.AluOpType
+ACT = mybir.ActivationFunctionType
+
+P = 128
+PACK = 4
+CH = 128
+NCH = S // CH
+GR = CH // D
+PAIR = 2 * CH
+EPS = 0.1
+W1_VECTOR_M = 44
+OUT_CHUNKS = [(0, 128), (128, 128), (256, 128), (384, 64), (448, 64)]
+
+
+def tile_picked_ygrp_none_po_kernel(
+    tc, x_words, x_scales, w1, w2, gam, offs, out_0, out_1, out_2
+):
+    nc = tc.nc
+    with ExitStack() as ctx:
+        sb = ctx.enter_context(tc.tile_pool(name="sb", bufs=1))
+        ps = ctx.enter_context(tc.psum_pool(name="ps", bufs=1))
+
+        offsets = sb.tile([P, S // 16], U16, name="offsets")
+        xw = sb.tile([P, T], I32, name="xw", align_bytes=64)
+        xs = sb.tile([P, T], U8, name="xs", align_bytes=64)
+        w1_raw = [sb.tile([P, PACK, H // 2], F32, name="w1_raw%d" % h, align_bytes=64) for h in range(2)]
+        w2_raw = [
+            sb.tile([P, PACK, N // 2], F32, name="w2_raw%d" % h, tag="w2_ee%d" % h, align_bytes=64) for h in range(2)
+        ]
+        gam_sb = sb.tile([P, PACK], F32, name="gam_sb")
+        ident = sb.tile([P, P], F32, name="ident", align_bytes=64)
+
+        nc.vector.memset(xs[:].bitcast(I32), 0)
+        nc.sync.dma_start(xw[:], x_words[0].rearrange("p n t -> p (n t)").bitcast(I32))
+        nc.sync.dma_start(offsets[:], offs)
+        for q in range(4):
+            nc.sync.dma_start(
+                xs[32 * q : 32 * q + 4, :].bitcast(I32), x_scales[0, 4 * q : 4 * q + 4, :].bitcast(I32)
+            )
+        for h in range(2):
+            nc.sync.dma_start(
+                w1_raw[h][:], w1.rearrange("(p j) c -> p j c", j=PACK)[:, :, h * H // 2 : (h + 1) * H // 2]
+            )
+        nc.sync.dma_start(gam_sb[:], gam.rearrange("(p t) o -> p (t o)", t=PACK))
+        for h in range(2):
+            nc.sync.dma_start(
+                w2_raw[h][:], w2.rearrange("(p j) c -> p j c", j=PACK)[:, :, h * N // 2 : (h + 1) * N // 2]
+            )
+        make_identity(nc, ident[:])
+        eps = sb.tile([P, 2], F32, name="eps")
+        nc.gpsimd.memset(eps[:, 0:1], 100.0)
+        nc.scalar.activation(eps[:, 1:2], eps[:, 0:1], ACT.Abs_reciprocal_sqrt)
+
+        xg = sb.tile([P, S], U32, name="xg", align_bytes=64)
+        nc.vector.tensor_copy(xg[:], xw[:].bitcast(U32).indirect(offsets[:]))
+        xgs = []
+        for g in range(2):
+            scales = sb.tile([P, PAIR], U8, name="xgs%d" % g, align_bytes=64)
+            nc.vector.tensor_copy(scales[:], xs[:].indirect(offsets[:, g * PAIR // 16 : (g + 1) * PAIR // 16]))
+            xgs.append(scales)
+
+        def dealt(raw, wb, m0, m1, base=0):
+            dst = wb[:].rearrange("p (t m j) -> p m t j", t=PACK, j=PACK)[:, m0:m1]
+            src = raw[:].rearrange("p j (m t) -> p m t j", t=PACK)[:, m0 - base : m1 - base]
+            return dst, src
+
+        w1q = sb.tile([P, H], U32, name="w1q", align_bytes=64)
+        w1s = sb.tile([P, H], U8, name="w1s", align_bytes=64)
+        for h in range(2):
+            w1b = sb.tile([P, PACK, H // 2], BF16, name="w1b%d" % h, align_bytes=64)
+            dst = w1b[:].rearrange("p t (m j) -> p m t j", j=PACK)
+            src = w1_raw[h][:].rearrange("p j (m t) -> p m t j", t=PACK)
+            if h == 0:
+                nc.scalar.copy(dst, src)
+            else:
+                nc.vector.tensor_copy(dst, src)
+            for t in range(PACK):
+                cols = slice(P * t + 64 * h, P * t + 64 * (h + 1))
+                nc.vector.quantize_mx(out=w1q[:, cols].bitcast(FP8X4), scales=w1s[:, cols], in_=w1b[:, t, :])
+
+        def product(acc, wq, ws, codes, scales):
+            for t in range(PACK):
+                nc.tensor.matmul_mx(
+                    out=acc[:, t, :],
+                    lhsT=wq[:, P * t : P * (t + 1)].bitcast(FP8X4),
+                    lhsT_scale=ws[:, P * t : P * (t + 1)],
+                    rhs=codes.bitcast(FP8X4),
+                    rhs_scale=scales,
+                    start=True,
+                    stop=True,
+                )
+
+        ys = []
+        for c in range(NCH):
+            y = ps.tile([P, PACK, CH], F32, name="y%d" % c, tag="bank%d" % c)
+            cols = slice(CH * (c % 2), CH * (c % 2 + 1))
+            product(y, w1q, w1s, xg[:, CH * c : CH * (c + 1)], xgs[c // 2][:, cols])
+            ys.append(y)
+
+        gam_rep = sb.tile([P, 2 * GR, PACK], F32, name="gam_rep", align_bytes=64)
+        gam_t = sb.tile([P, P], F32, name="gam_t")
+        gam_ps = ps.tile([P, P], F32, name="gam_ps", tag="bank5")
+        nc.scalar.copy(gam_rep[:], gam_sb[:].unsqueeze(1).to_broadcast([P, 2 * GR, PACK]))
+        nc.tensor.transpose(gam_ps[:], gam_rep[:].rearrange("p v t -> p (v t)"), ident[:])
+        nc.scalar.copy(gam_t[:], gam_ps[:])
+
+        w2b = sb.tile([P, PACK * N], BF16, name="w2b", align_bytes=64)
+        w2q = sb.tile([P, N], U32, name="w2q", align_bytes=64)
+        w2s = sb.tile([P, N], U8, name="w2s", align_bytes=64)
+        for h in range(2):
+            nc.scalar.copy(*dealt(w2_raw[h], w2b, 64 * h, 64 * (h + 1), 64 * h))
+        ee = [sb.tile([P, D // 2, 2 * GR * PACK], F32, name="ee%d" % h, tag="w2_ee%d" % h, align_bytes=64) for h in range(2)]
+        half = GR * PACK
+
+        def centre(c):
+            sums = sb.tile([P, GR, PACK], F32, name="sums%d" % c)
+            mean = sb.tile([P, GR, PACK], F32, name="mean%d" % c)
+            dd = sb.tile([P, GR, D, PACK], F32, name="dd%d" % c)
+            nc.vector.tensor_reduce(
+                out=sums[:], in_=ys[c][:].rearrange("p t (v d) -> p v t d", d=D), axis=mybir.AxisListType.X, op=ALU.add
+            )
+            nc.gpsimd.tensor_scalar(mean[:], sums[:], 1.0 / D, 0.0, ALU.mult, ALU.add)
+            nc.vector.tensor_tensor(
+                dd[:],
+                ys[c][:].rearrange("p t (v d) -> p v d t", d=D),
+                mean[:].unsqueeze(2).to_broadcast([P, GR, D, PACK]),
+                ALU.subtract,
+            )
+            return dd
+
+        dds = []
+        for c in range(2):
+            dd = centre(c)
+            for h in range(2):
+                nc.scalar.activation(
+                    ee[h][:, :, half * c : half * (c + 1)].rearrange("p d (v t) -> p d v t", t=PACK),
+                    dd[:].rearrange("p v d t -> p d v t")[:, 4 * h : 4 * (h + 1)],
+                    ACT.Square,
+                )
+            dds.append(dd)
+
+        st = ps.tile([P, 2, P], F32, name="st", tag="bank4")
+        for d in range(D):
+            nc.tensor.matmul(
+                st[:, 0, :], ee[d // 4][:, d % 4, :], ident[:], start=(d == 0), stop=(d == D - 1), is_transpose=True
+            )
+        rt = sb.tile([P, P], F32, name="rt", align_bytes=64)
+        nc.scalar.activation(rt[:], st[:, 0, :], ACT.Abs_reciprocal_sqrt, bias=eps[:, 1:2], scale=1.0 / D)
+        rg0 = sb.tile([P, P], F32, name="rg0", align_bytes=64)
+        nc.gpsimd.tensor_tensor(rg0[:], rt[:], gam_t[:], ALU.mult)
+        nc.tensor.transpose(st[:, 1, :], rg0[:], ident[:])
+
+        sqs = []
+        for c in range(2, 4):
+            dd = centre(c)
+            if c == 2:
+                sq = sb.tile([P, 2 * GR, PACK, 4], F32, name="sq2", align_bytes=64)
+            else:
+                sq = sb.tile([P, 2 * GR, PACK, 4], F32, name="sq3", tag="w2_ee1", align_bytes=64)
+            nc.scalar.activation(sq[:], dd[:].rearrange("p v (h i) t -> p (v h) t i", i=4), ACT.Square)
+            sqs.append(sq)
+            dds.append(dd)
+
+        nc.vector.quantize_mx(out=w2q[:].bitcast(FP8X4), scales=w2s[:], in_=w2b[:])
+
+        oq = sb.tile([P, S], U32, name="oq", align_bytes=64)
+        osc = sb.tile([P, S], U8, name="osc", align_bytes=64)
+        out_rows = out_0.rearrange("(p t) n -> p t n", t=PACK)
+        out_words = out_1[0].rearrange("p n t -> p (n t)").bitcast(I32)
+        outs = []
+
+        def second(i, rg):
+            c0, w = OUT_CHUNKS[i]
+            c, v0, nv = c0 // CH, (c0 % CH) // D, w // D
+            zb = sb.tile([P, nv, D, PACK], BF16, name="zb%d" % i, align_bytes=64)
+            zq = sb.tile([P, w], U32, name="zq%d" % i, align_bytes=64)
+            zs = sb.tile([P, w], U8, name="zs%d" % i, align_bytes=64)
+            r0 = GR * (c % 2) + v0
+            nc.vector.tensor_tensor(
+                zb[:],
+                dds[c][:, v0 : v0 + nv],
+                rg[:, r0 : r0 + nv, :].unsqueeze(2).to_broadcast([P, nv, D, PACK]),
+                ALU.mult,
+            )
+            nc.vector.quantize_mx(
+                out=zq[:].bitcast(FP8X4), scales=zs[:], in_=zb[:].rearrange("p v d t -> p (v d t)")
+            )
+            o = ps.tile([P, PACK, w], F32, name="o%d" % i, tag="bank%d" % ((5 + i) % 8))
+            product(o, w2q, w2s, zq[:], zs[:])
+            outs.append(o)
+
+        for i in range(2):
+            second(i, st[:, 1, :].rearrange("p (v t) -> p v t", t=PACK))
+
+        ssq = sb.tile([P, 2 * GR, PACK], F32, name="ssq")
+        for h in range(2):
+            nc.vector.tensor_reduce(
+                out=ssq[:, GR * h : GR * (h + 1), :],
+                in_=sqs[h][:].rearrange("p (v h) t i -> p v t h i", h=2),
+                axis=mybir.AxisListType.XY,
+                op=ALU.add,
+            )
+        r1 = sb.tile([P, 2 * GR, PACK], F32, name="r1")
+        rg1 = sb.tile([P, 2 * GR, PACK], F32, name="rg1")
+        nc.scalar.activation(r1[:], ssq[:], ACT.Abs_reciprocal_sqrt, bias=eps[:, 1:2], scale=1.0 / D)
+        nc.gpsimd.tensor_tensor(rg1[:], r1[:], gam_rep[:], ALU.mult)
+        for i in range(2, 5):
+            second(i, rg1[:])
+
+        ob = sb.tile([P, S, PACK], BF16, name="ob", align_bytes=64)
+
+        def planes(c0, c1):
+            nc.vector.quantize_mx(
+                out=oq[:, c0:c1].bitcast(FP8X4),
+                scales=osc[:, c0:c1],
+                in_=ob[:, c0:c1, :].rearrange("p n t -> p (n t)"),
+            )
+
+        for i, (c0, w) in enumerate(OUT_CHUNKS):
+            o = outs[i]
+            cols = slice(c0, c0 + w)
+            o32 = sb.tile([P, PACK, w], F32, name="o32_%d" % i)
+            if i == 4:
+                nc.vector.tensor_copy(ob[:, cols, :], o[:].rearrange("p t n -> p n t"))
+            nc.scalar.copy(o32[:], o[:])
+            nc.sync.dma_start(out_rows[:, :, cols], o32[:])
+            if i < 2:
+                nc.scalar.copy(ob[:, cols, :], o[:].rearrange("p t n -> p n t"))
+            elif i < 4:
+                nc.vector.tensor_copy(
+                    ob[:, cols, :].rearrange("p (a i) t -> p a t i", i=4),
+                    o32[:].rearrange("p t (a i) -> p a t i", i=4),
+                )
+            if i == 1:
+                planes(0, 256)
+                nc.sync.dma_start(out_words[:, 0:256], oq[:, 0:256].bitcast(I32))
+            if i == 2:
+                planes(256, 384)
+            if i == 4:
+                planes(384, 512)
+                nc.scalar.dma_start(out_words[:, 256:512], oq[:, 256:512].bitcast(I32))
+        for q in range(4):
+            eng = nc.sync if q % 2 == 0 else nc.scalar
+            eng.dma_start(out_2[0, 4 * q : 4 * q + 4, :].bitcast(I32), osc[32 * q : 32 * q + 4, :].bitcast(I32))

@@ -15,16 +15,21 @@ U8 = mybir.dt.uint8
 FP8X4 = mybir.dt.float8_e4m3fn_x4
 ALU = mybir.AluOpType
 ACT = mybir.ActivationFunctionType
+AXIS = mybir.AxisListType
 
 P = 128
 PACK = 4
-CH = 128
-NCH = S // CH
-GR = CH // D
-PAIR = 2 * CH
-EPS = 0.1
-W1_VECTOR_M = 44
-OUT_CHUNKS = [(0, 128), (128, 128), (256, 128), (384, 64), (448, 64)]
+LIST_ROWS = 16
+QUADRANT = 32
+CHUNK = 128
+PAIR = 2 * CHUNK
+GROUPS = CHUNK // D
+STATS = GROUPS * PACK
+HALF_D = D // 2
+HALF_M = P // 2
+ALIGN = 64
+INV_SQUARE_EPS = 100.0
+PIECES = [(256, 128), (384, 128), (0, 128), (128, 64), (192, 64)]
 
 
 def tile_picked_ygrp_none_po_kernel(
@@ -35,22 +40,24 @@ def tile_picked_ygrp_none_po_kernel(
         sb = ctx.enter_context(tc.tile_pool(name="sb", bufs=1))
         ps = ctx.enter_context(tc.psum_pool(name="ps", bufs=1))
 
-        offsets = sb.tile([P, S // 16], U16, name="offsets")
-        xw = sb.tile([P, T], I32, name="xw", align_bytes=64)
-        xs = sb.tile([P, T], U8, name="xs", align_bytes=64)
-        w1_raw = [sb.tile([P, PACK, H // 2], F32, name="w1_raw%d" % h, align_bytes=64) for h in range(2)]
+        offsets = sb.tile([P, S // LIST_ROWS], U16, name="offsets")
+        xw = sb.tile([P, T], I32, name="xw", align_bytes=ALIGN)
+        xs = sb.tile([P, T], U8, name="xs", align_bytes=ALIGN)
+        w1_raw = [sb.tile([P, PACK, H // 2], F32, name="w1_raw%d" % h, align_bytes=ALIGN) for h in range(2)]
         w2_raw = [
-            sb.tile([P, PACK, N // 2], F32, name="w2_raw%d" % h, tag="w2_ee%d" % h, align_bytes=64) for h in range(2)
+            sb.tile([P, PACK, N // 2], F32, name="w2_raw%d" % h, tag="w2_raw%d" % h, align_bytes=ALIGN)
+            for h in range(2)
         ]
         gam_sb = sb.tile([P, PACK], F32, name="gam_sb")
-        ident = sb.tile([P, P], F32, name="ident", align_bytes=64)
+        ident = sb.tile([P, P], F32, name="ident", align_bytes=ALIGN)
 
         nc.vector.memset(xs[:].bitcast(I32), 0)
         nc.sync.dma_start(xw[:], x_words[0].rearrange("p n t -> p (n t)").bitcast(I32))
         nc.sync.dma_start(offsets[:], offs)
-        for q in range(4):
+        for q in range(P // QUADRANT):
             nc.sync.dma_start(
-                xs[32 * q : 32 * q + 4, :].bitcast(I32), x_scales[0, 4 * q : 4 * q + 4, :].bitcast(I32)
+                xs[QUADRANT * q : QUADRANT * q + PACK, :].bitcast(I32),
+                x_scales[0, PACK * q : PACK * (q + 1), :].bitcast(I32),
             )
         for h in range(2):
             nc.sync.dma_start(
@@ -62,35 +69,31 @@ def tile_picked_ygrp_none_po_kernel(
                 w2_raw[h][:], w2.rearrange("(p j) c -> p j c", j=PACK)[:, :, h * N // 2 : (h + 1) * N // 2]
             )
         make_identity(nc, ident[:])
-        eps = sb.tile([P, 2], F32, name="eps")
-        nc.gpsimd.memset(eps[:, 0:1], 100.0)
-        nc.scalar.activation(eps[:, 1:2], eps[:, 0:1], ACT.Abs_reciprocal_sqrt)
 
-        xg = sb.tile([P, S], U32, name="xg", align_bytes=64)
+        eps_cols = sb.tile([P, 2], F32, name="eps_cols")
+        nc.gpsimd.memset(eps_cols[:, 0:1], INV_SQUARE_EPS)
+        nc.scalar.activation(eps_cols[:, 1:2], eps_cols[:, 0:1], ACT.Abs_reciprocal_sqrt)
+        eps = eps_cols[:, 1:2]
+
+        xg = sb.tile([P, S], U32, name="xg", align_bytes=ALIGN)
         nc.vector.tensor_copy(xg[:], xw[:].bitcast(U32).indirect(offsets[:]))
         xgs = []
-        for g in range(2):
-            scales = sb.tile([P, PAIR], U8, name="xgs%d" % g, align_bytes=64)
-            nc.vector.tensor_copy(scales[:], xs[:].indirect(offsets[:, g * PAIR // 16 : (g + 1) * PAIR // 16]))
-            xgs.append(scales)
+        for g in range(S // PAIR):
+            picked = sb.tile([P, PAIR], U8, name="xgs%d" % g, align_bytes=ALIGN)
+            entries = offsets[:, g * PAIR // LIST_ROWS : (g + 1) * PAIR // LIST_ROWS]
+            nc.vector.tensor_copy(picked[:], xs[:].indirect(entries))
+            xgs.append(picked)
 
-        def dealt(raw, wb, m0, m1, base=0):
-            dst = wb[:].rearrange("p (t m j) -> p m t j", t=PACK, j=PACK)[:, m0:m1]
-            src = raw[:].rearrange("p j (m t) -> p m t j", t=PACK)[:, m0 - base : m1 - base]
-            return dst, src
+        def dealt(raw):
+            return raw[:].rearrange("p j (m t) -> p m t j", t=PACK)
 
-        w1q = sb.tile([P, H], U32, name="w1q", align_bytes=64)
-        w1s = sb.tile([P, H], U8, name="w1s", align_bytes=64)
-        for h in range(2):
-            w1b = sb.tile([P, PACK, H // 2], BF16, name="w1b%d" % h, align_bytes=64)
-            dst = w1b[:].rearrange("p t (m j) -> p m t j", j=PACK)
-            src = w1_raw[h][:].rearrange("p j (m t) -> p m t j", t=PACK)
-            if h == 0:
-                nc.scalar.copy(dst, src)
-            else:
-                nc.vector.tensor_copy(dst, src)
+        w1q = sb.tile([P, H], U32, name="w1q", align_bytes=ALIGN)
+        w1s = sb.tile([P, H], U8, name="w1s", align_bytes=ALIGN)
+        for h, cast in enumerate((nc.scalar.copy, nc.vector.tensor_copy)):
+            w1b = sb.tile([P, PACK, H // 2], BF16, name="w1b%d" % h, align_bytes=ALIGN)
+            cast(w1b[:].rearrange("p t (m j) -> p m t j", j=PACK), dealt(w1_raw[h]))
             for t in range(PACK):
-                cols = slice(P * t + 64 * h, P * t + 64 * (h + 1))
+                cols = slice(P * t + HALF_M * h, P * t + HALF_M * (h + 1))
                 nc.vector.quantize_mx(out=w1q[:, cols].bitcast(FP8X4), scales=w1s[:, cols], in_=w1b[:, t, :])
 
         def product(acc, wq, ws, codes, scales):
@@ -106,154 +109,169 @@ def tile_picked_ygrp_none_po_kernel(
                 )
 
         ys = []
-        for c in range(NCH):
-            y = ps.tile([P, PACK, CH], F32, name="y%d" % c, tag="bank%d" % c)
-            cols = slice(CH * (c % 2), CH * (c % 2 + 1))
-            product(y, w1q, w1s, xg[:, CH * c : CH * (c + 1)], xgs[c // 2][:, cols])
+        for c in range(S // CHUNK):
+            y = ps.tile([P, PACK, CHUNK], F32, name="y%d" % c, tag="bank%d" % c)
+            in_pair = slice(CHUNK * (c % 2), CHUNK * (c % 2 + 1))
+            product(y, w1q, w1s, xg[:, CHUNK * c : CHUNK * (c + 1)], xgs[c // 2][:, in_pair])
             ys.append(y)
 
-        gam_rep = sb.tile([P, 2 * GR, PACK], F32, name="gam_rep", align_bytes=64)
-        gam_t = sb.tile([P, P], F32, name="gam_t")
-        gam_ps = ps.tile([P, P], F32, name="gam_ps", tag="bank5")
-        nc.scalar.copy(gam_rep[:], gam_sb[:].unsqueeze(1).to_broadcast([P, 2 * GR, PACK]))
-        nc.tensor.transpose(gam_ps[:], gam_rep[:].rearrange("p v t -> p (v t)"), ident[:])
-        nc.scalar.copy(gam_t[:], gam_ps[:])
-
-        w2b = sb.tile([P, PACK * N], BF16, name="w2b", align_bytes=64)
-        w2q = sb.tile([P, N], U32, name="w2q", align_bytes=64)
-        w2s = sb.tile([P, N], U8, name="w2s", align_bytes=64)
+        w2b = sb.tile([P, PACK * N], BF16, name="w2b", align_bytes=ALIGN)
+        w2q = sb.tile([P, N], U32, name="w2q", align_bytes=ALIGN)
+        w2s = sb.tile([P, N], U8, name="w2s", align_bytes=ALIGN)
         for h in range(2):
-            nc.scalar.copy(*dealt(w2_raw[h], w2b, 64 * h, 64 * (h + 1), 64 * h))
-        ee = [sb.tile([P, D // 2, 2 * GR * PACK], F32, name="ee%d" % h, tag="w2_ee%d" % h, align_bytes=64) for h in range(2)]
-        half = GR * PACK
+            nc.scalar.copy(
+                w2b[:].rearrange("p (t m j) -> p m t j", t=PACK, j=PACK)[:, HALF_M * h : HALF_M * (h + 1)],
+                dealt(w2_raw[h]),
+            )
 
-        def centre(c):
-            sums = sb.tile([P, GR, PACK], F32, name="sums%d" % c)
-            mean = sb.tile([P, GR, PACK], F32, name="mean%d" % c)
-            dd = sb.tile([P, GR, D, PACK], F32, name="dd%d" % c)
+        def group_means(c):
+            sums = sb.tile([P, GROUPS, PACK], F32, name="sums%d" % c)
+            mean = sb.tile([P, GROUPS, PACK], F32, name="mean%d" % c)
             nc.vector.tensor_reduce(
-                out=sums[:], in_=ys[c][:].rearrange("p t (v d) -> p v t d", d=D), axis=mybir.AxisListType.X, op=ALU.add
+                out=sums[:], in_=ys[c][:].rearrange("p t (v d) -> p v t d", d=D), axis=AXIS.X, op=ALU.add
             )
             nc.gpsimd.tensor_scalar(mean[:], sums[:], 1.0 / D, 0.0, ALU.mult, ALU.add)
+            return mean
+
+        def centre(c, mean):
+            dd = sb.tile([P, GROUPS, D, PACK], F32, name="dd%d" % c, tag="dd%d" % c, align_bytes=ALIGN)
             nc.vector.tensor_tensor(
                 dd[:],
                 ys[c][:].rearrange("p t (v d) -> p v d t", d=D),
-                mean[:].unsqueeze(2).to_broadcast([P, GR, D, PACK]),
+                mean[:].unsqueeze(2).to_broadcast([P, GROUPS, D, PACK]),
                 ALU.subtract,
             )
             return dd
 
+        ee = [
+            sb.tile([P, HALF_D, 2 * STATS], F32, name="ee%d" % h, tag="w2_raw%d" % h, align_bytes=ALIGN)
+            for h in range(2)
+        ]
         dds = []
-        for c in range(2):
-            dd = centre(c)
+        means = [group_means(c) for c in (0, 1)]
+        for c in (0, 1):
+            dds.append(centre(c, means[c]))
             for h in range(2):
                 nc.scalar.activation(
-                    ee[h][:, :, half * c : half * (c + 1)].rearrange("p d (v t) -> p d v t", t=PACK),
-                    dd[:].rearrange("p v d t -> p d v t")[:, 4 * h : 4 * (h + 1)],
+                    ee[h][:, :, STATS * c : STATS * (c + 1)].rearrange("p d (v t) -> p d v t", t=PACK),
+                    dds[c][:].rearrange("p v d t -> p d v t")[:, HALF_D * h : HALF_D * (h + 1)],
                     ACT.Square,
                 )
-            dds.append(dd)
-
-        st = ps.tile([P, 2, P], F32, name="st", tag="bank4")
+        turned = ps.tile([P, 2, P], F32, name="turned", tag="bank4")
         for d in range(D):
             nc.tensor.matmul(
-                st[:, 0, :], ee[d // 4][:, d % 4, :], ident[:], start=(d == 0), stop=(d == D - 1), is_transpose=True
+                turned[:, 0, :],
+                ee[d // HALF_D][:, d % HALF_D, :],
+                ident[:],
+                start=(d == 0),
+                stop=(d == D - 1),
+                is_transpose=True,
             )
-        rt = sb.tile([P, P], F32, name="rt", align_bytes=64)
-        nc.scalar.activation(rt[:], st[:, 0, :], ACT.Abs_reciprocal_sqrt, bias=eps[:, 1:2], scale=1.0 / D)
-        rg0 = sb.tile([P, P], F32, name="rg0", align_bytes=64)
-        nc.gpsimd.tensor_tensor(rg0[:], rt[:], gam_t[:], ALU.mult)
-        nc.tensor.transpose(st[:, 1, :], rg0[:], ident[:])
 
-        sqs = []
-        for c in range(2, 4):
-            dd = centre(c)
-            if c == 2:
-                sq = sb.tile([P, 2 * GR, PACK, 4], F32, name="sq2", align_bytes=64)
-            else:
-                sq = sb.tile([P, 2 * GR, PACK, 4], F32, name="sq3", tag="w2_ee1", align_bytes=64)
-            nc.scalar.activation(sq[:], dd[:].rearrange("p v (h i) t -> p (v h) t i", i=4), ACT.Square)
-            sqs.append(sq)
-            dds.append(dd)
+        squares = []
+        means = [group_means(c) for c in (2, 3)]
+        for c in (2, 3):
+            dds.append(centre(c, means[c - 2]))
+            sq = sb.tile([P, 2 * GROUPS, PACK, HALF_D], F32, name="sq%d" % c)
+            nc.scalar.activation(sq[:], dds[c][:].rearrange("p v (h i) t -> p (v h) t i", i=HALF_D), ACT.Square)
+            squares.append(sq)
 
         nc.vector.quantize_mx(out=w2q[:].bitcast(FP8X4), scales=w2s[:], in_=w2b[:])
 
-        oq = sb.tile([P, S], U32, name="oq", align_bytes=64)
-        osc = sb.tile([P, S], U8, name="osc", align_bytes=64)
-        out_rows = out_0.rearrange("(p t) n -> p t n", t=PACK)
-        out_words = out_1[0].rearrange("p n t -> p (n t)").bitcast(I32)
+        def with_gain(name, tag, inv_dev, groups):
+            factor = sb.tile([P, groups, PACK], F32, name=name, tag=tag, align_bytes=ALIGN)
+            nc.vector.tensor_tensor(
+                factor[:], inv_dev, gam_sb[:].unsqueeze(1).to_broadcast([P, groups, PACK]), ALU.mult
+            )
+            return factor
+
+        factors = {}
+        for c in (2, 3):
+            ssq = sb.tile([P, GROUPS, PACK], F32, name="ssq%d" % c, tag="ssq%d" % c, align_bytes=ALIGN)
+            inv_dev = sb.tile([P, GROUPS, PACK], F32, name="inv_dev%d" % c)
+            nc.vector.tensor_reduce(
+                out=ssq[:], in_=squares[c - 2][:].rearrange("p (v h) t i -> p v t h i", h=2), axis=AXIS.XY, op=ALU.add
+            )
+            nc.scalar.activation(inv_dev[:], ssq[:], ACT.Abs_reciprocal_sqrt, bias=eps, scale=1.0 / D)
+            factors[c] = with_gain("factor%d" % c, "factor%d" % c, inv_dev[:], GROUPS)[:]
+
+        inv_dev_turned = sb.tile([P, P], F32, name="inv_dev_turned", tag="ssq2", align_bytes=ALIGN)
+        nc.scalar.activation(inv_dev_turned[:], turned[:, 0, :], ACT.Abs_reciprocal_sqrt, bias=eps, scale=1.0 / D)
+        nc.tensor.transpose(turned[:, 1, :], inv_dev_turned[:], ident[:])
+
         outs = []
 
-        def second(i, rg):
-            c0, w = OUT_CHUNKS[i]
-            c, v0, nv = c0 // CH, (c0 % CH) // D, w // D
-            zb = sb.tile([P, nv, D, PACK], BF16, name="zb%d" % i, align_bytes=64)
-            zq = sb.tile([P, w], U32, name="zq%d" % i, align_bytes=64)
-            zs = sb.tile([P, w], U8, name="zs%d" % i, align_bytes=64)
-            r0 = GR * (c % 2) + v0
+        def second_layer(i, z_tag):
+            first, width = PIECES[i]
+            c, v0, groups = first // CHUNK, (first % CHUNK) // D, width // D
+            zb = sb.tile([P, groups, D, PACK], BF16, name="zb%d" % i, tag=z_tag, align_bytes=ALIGN)
+            zq = sb.tile([P, width], U32, name="zq%d" % i, align_bytes=ALIGN)
+            zs = sb.tile([P, width], U8, name="zs%d" % i, align_bytes=ALIGN)
             nc.vector.tensor_tensor(
                 zb[:],
-                dds[c][:, v0 : v0 + nv],
-                rg[:, r0 : r0 + nv, :].unsqueeze(2).to_broadcast([P, nv, D, PACK]),
+                dds[c][:, v0 : v0 + groups],
+                factors[c][:, v0 : v0 + groups, :].unsqueeze(2).to_broadcast([P, groups, D, PACK]),
                 ALU.mult,
             )
+            nc.vector.quantize_mx(out=zq[:].bitcast(FP8X4), scales=zs[:], in_=zb[:].rearrange("p v d t -> p (v d t)"))
+            acc = ps.tile([P, PACK, width], F32, name="acc%d" % i, tag="bank%d" % ((5 + i) % 8))
+            product(acc, w2q, w2s, zq[:], zs[:])
+            outs.append(acc)
+
+        second_layer(0, "zb_first")
+        second_layer(1, "zb_first")
+        factor01 = with_gain("factor01", "dd2", turned[:, 1, :].rearrange("p (v t) -> p v t", t=PACK), 2 * GROUPS)
+        factors[0], factors[1] = factor01[:, 0:GROUPS, :], factor01[:, GROUPS : 2 * GROUPS, :]
+        for i in range(2, len(PIECES)):
+            second_layer(i, "zb%d" % i)
+
+        ob = sb.tile([P, S, PACK], BF16, name="ob", align_bytes=ALIGN)
+        oq = sb.tile([P, S], U32, name="oq", align_bytes=ALIGN)
+        osc = sb.tile([P, S], U8, name="osc", align_bytes=ALIGN)
+        out_rows = out_0.rearrange("(p t) n -> p t n", t=PACK)
+        out_words = out_1[0].rearrange("p n t -> p (n t)").bitcast(I32)
+        last = len(PIECES) - 1
+
+        def round_from_bank(copy, i):
+            first, width = PIECES[i]
+            copy(ob[:, first : first + width, :], outs[i][:].rearrange("p t n -> p n t"))
+
+        def planes(first, end):
             nc.vector.quantize_mx(
-                out=zq[:].bitcast(FP8X4), scales=zs[:], in_=zb[:].rearrange("p v d t -> p (v d t)")
-            )
-            o = ps.tile([P, PACK, w], F32, name="o%d" % i, tag="bank%d" % ((5 + i) % 8))
-            product(o, w2q, w2s, zq[:], zs[:])
-            outs.append(o)
-
-        for i in range(2):
-            second(i, st[:, 1, :].rearrange("p (v t) -> p v t", t=PACK))
-
-        ssq = sb.tile([P, 2 * GR, PACK], F32, name="ssq")
-        for h in range(2):
-            nc.vector.tensor_reduce(
-                out=ssq[:, GR * h : GR * (h + 1), :],
-                in_=sqs[h][:].rearrange("p (v h) t i -> p v t h i", h=2),
-                axis=mybir.AxisListType.XY,
-                op=ALU.add,
-            )
-        r1 = sb.tile([P, 2 * GR, PACK], F32, name="r1")
-        rg1 = sb.tile([P, 2 * GR, PACK], F32, name="rg1")
-        nc.scalar.activation(r1[:], ssq[:], ACT.Abs_reciprocal_sqrt, bias=eps[:, 1:2], scale=1.0 / D)
-        nc.gpsimd.tensor_tensor(rg1[:], r1[:], gam_rep[:], ALU.mult)
-        for i in range(2, 5):
-            second(i, rg1[:])
-
-        ob = sb.tile([P, S, PACK], BF16, name="ob", align_bytes=64)
-
-        def planes(c0, c1):
-            nc.vector.quantize_mx(
-                out=oq[:, c0:c1].bitcast(FP8X4),
-                scales=osc[:, c0:c1],
-                in_=ob[:, c0:c1, :].rearrange("p n t -> p (n t)"),
+                out=oq[:, first:end].bitcast(FP8X4),
+                scales=osc[:, first:end],
+                in_=ob[:, first:end, :].rearrange("p n t -> p (n t)"),
             )
 
-        for i, (c0, w) in enumerate(OUT_CHUNKS):
-            o = outs[i]
-            cols = slice(c0, c0 + w)
-            o32 = sb.tile([P, PACK, w], F32, name="o32_%d" % i)
-            if i == 4:
-                nc.vector.tensor_copy(ob[:, cols, :], o[:].rearrange("p t n -> p n t"))
-            nc.scalar.copy(o32[:], o[:])
-            nc.sync.dma_start(out_rows[:, :, cols], o32[:])
-            if i < 2:
-                nc.scalar.copy(ob[:, cols, :], o[:].rearrange("p t n -> p n t"))
-            elif i < 4:
-                nc.vector.tensor_copy(
-                    ob[:, cols, :].rearrange("p (a i) t -> p a t i", i=4),
-                    o32[:].rearrange("p t (a i) -> p a t i", i=4),
-                )
-            if i == 1:
-                planes(0, 256)
-                nc.sync.dma_start(out_words[:, 0:256], oq[:, 0:256].bitcast(I32))
+        staged = []
+        for i, (first, width) in enumerate(PIECES):
+            if first % CHUNK == 0:
+                o32 = sb.tile([P, PACK, CHUNK], F32, name="o32_%d" % i)
+            part = o32[:, :, first % CHUNK : first % CHUNK + width]
+            if i == last:
+                round_from_bank(nc.vector.tensor_copy, i)
+            nc.scalar.copy(part, outs[i][:])
+            if (first + width) % CHUNK == 0:
+                nc.sync.dma_start(out_rows[:, :, first + width - CHUNK : first + width], o32[:])
+            staged.append(part)
+
+        for i in (0, 1):
+            round_from_bank(nc.scalar.copy, i)
+        planes(PAIR, S)
+        nc.sync.dma_start(out_words[:, PAIR:S], oq[:, PAIR:S].bitcast(I32))
+        for i in (2, 3):
+            first, width = PIECES[i]
+            nc.vector.tensor_copy(
+                ob[:, first : first + width, :].rearrange("p (a i) t -> p a t i", i=4),
+                staged[i].rearrange("p t (a i) -> p a t i", i=4),
+            )
             if i == 2:
-                planes(256, 384)
-            if i == 4:
-                planes(384, 512)
-                nc.scalar.dma_start(out_words[:, 256:512], oq[:, 256:512].bitcast(I32))
-        for q in range(4):
-            eng = nc.sync if q % 2 == 0 else nc.scalar
-            eng.dma_start(out_2[0, 4 * q : 4 * q + 4, :].bitcast(I32), osc[32 * q : 32 * q + 4, :].bitcast(I32))
+                planes(0, CHUNK)
+        planes(CHUNK, PAIR)
+        nc.sync.dma_start(out_words[:, 0:PAIR], oq[:, 0:PAIR].bitcast(I32))
+        for q in range(P // QUADRANT):
+            queue = nc.sync if q % 2 == 0 else nc.scalar
+            queue.dma_start(
+                out_2[0, PACK * q : PACK * (q + 1), :].bitcast(I32),
+                osc[QUADRANT * q : QUADRANT * q + PACK, :].bitcast(I32),
+            )

from contextlib import ExitStack

import concourse.mybir as mybir
from concourse.masks import make_identity

K, T, S, H, N, D = 512, 1024, 512, 512, 512, 8
FLOPS = 2 * K * H * S + 2 * H * N * S

F32 = mybir.dt.float32
BF16 = mybir.dt.bfloat16
I32 = mybir.dt.int32
U32 = mybir.dt.uint32
U16 = mybir.dt.uint16
U8 = mybir.dt.uint8
FP8X4 = mybir.dt.float8_e4m3fn_x4
ALU = mybir.AluOpType
ACT = mybir.ActivationFunctionType
AXIS = mybir.AxisListType

P = 128
PACK = 4
LIST_ROWS = 16
QUADRANT = 32
CHUNK = 128
PAIR = 2 * CHUNK
GROUPS = CHUNK // D
STATS = GROUPS * PACK
HALF_D = D // 2
HALF_M = P // 2
ALIGN = 64
INV_SQUARE_EPS = 100.0
PIECES = [(256, 128), (384, 128), (0, 128), (128, 64), (192, 64)]


def tile_picked_ygrp_none_po_kernel(
    tc, x_words, x_scales, w1, w2, gam, offs, out_0, out_1, out_2
):
    nc = tc.nc
    with ExitStack() as ctx:
        sb = ctx.enter_context(tc.tile_pool(name="sb", bufs=1))
        ps = ctx.enter_context(tc.psum_pool(name="ps", bufs=1))

        offsets = sb.tile([P, S // LIST_ROWS], U16, name="offsets")
        xw = sb.tile([P, T], I32, name="xw", align_bytes=ALIGN)
        xs = sb.tile([P, T], U8, name="xs", align_bytes=ALIGN)
        w1_raw = [sb.tile([P, PACK, H // 2], F32, name="w1_raw%d" % h, align_bytes=ALIGN) for h in range(2)]
        w2_raw = [
            sb.tile([P, PACK, N // 2], F32, name="w2_raw%d" % h, tag="w2_raw%d" % h, align_bytes=ALIGN)
            for h in range(2)
        ]
        gam_sb = sb.tile([P, PACK], F32, name="gam_sb")
        ident = sb.tile([P, P], F32, name="ident", align_bytes=ALIGN)

        nc.vector.memset(xs[:].bitcast(I32), 0)
        nc.sync.dma_start(xw[:], x_words[0].rearrange("p n t -> p (n t)").bitcast(I32))
        nc.sync.dma_start(offsets[:], offs)
        for q in range(P // QUADRANT):
            nc.sync.dma_start(
                xs[QUADRANT * q : QUADRANT * q + PACK, :].bitcast(I32),
                x_scales[0, PACK * q : PACK * (q + 1), :].bitcast(I32),
            )
        for h in range(2):
            nc.sync.dma_start(
                w1_raw[h][:], w1.rearrange("(p j) c -> p j c", j=PACK)[:, :, h * H // 2 : (h + 1) * H // 2]
            )
        nc.sync.dma_start(gam_sb[:], gam.rearrange("(p t) o -> p (t o)", t=PACK))
        for h in range(2):
            nc.sync.dma_start(
                w2_raw[h][:], w2.rearrange("(p j) c -> p j c", j=PACK)[:, :, h * N // 2 : (h + 1) * N // 2]
            )
        make_identity(nc, ident[:])

        eps_cols = sb.tile([P, 2], F32, name="eps_cols")
        nc.gpsimd.memset(eps_cols[:, 0:1], INV_SQUARE_EPS)
        nc.scalar.activation(eps_cols[:, 1:2], eps_cols[:, 0:1], ACT.Abs_reciprocal_sqrt)
        eps = eps_cols[:, 1:2]

        xg = sb.tile([P, S], U32, name="xg", align_bytes=ALIGN)
        nc.vector.tensor_copy(xg[:], xw[:].bitcast(U32).indirect(offsets[:]))
        xgs = []
        for g in range(S // PAIR):
            picked = sb.tile([P, PAIR], U8, name="xgs%d" % g, align_bytes=ALIGN)
            entries = offsets[:, g * PAIR // LIST_ROWS : (g + 1) * PAIR // LIST_ROWS]
            nc.vector.tensor_copy(picked[:], xs[:].indirect(entries))
            xgs.append(picked)

        def dealt(raw):
            return raw[:].rearrange("p j (m t) -> p m t j", t=PACK)

        w1q = sb.tile([P, H], U32, name="w1q", align_bytes=ALIGN)
        w1s = sb.tile([P, H], U8, name="w1s", align_bytes=ALIGN)
        for h, cast in enumerate((nc.scalar.copy, nc.vector.tensor_copy)):
            w1b = sb.tile([P, PACK, H // 2], BF16, name="w1b%d" % h, align_bytes=ALIGN)
            cast(w1b[:].rearrange("p t (m j) -> p m t j", j=PACK), dealt(w1_raw[h]))
            for t in range(PACK):
                cols = slice(P * t + HALF_M * h, P * t + HALF_M * (h + 1))
                nc.vector.quantize_mx(out=w1q[:, cols].bitcast(FP8X4), scales=w1s[:, cols], in_=w1b[:, t, :])

        def product(acc, wq, ws, codes, scales):
            for t in range(PACK):
                nc.tensor.matmul_mx(
                    out=acc[:, t, :],
                    lhsT=wq[:, P * t : P * (t + 1)].bitcast(FP8X4),
                    lhsT_scale=ws[:, P * t : P * (t + 1)],
                    rhs=codes.bitcast(FP8X4),
                    rhs_scale=scales,
                    start=True,
                    stop=True,
                )

        ys = []
        for c in range(S // CHUNK):
            y = ps.tile([P, PACK, CHUNK], F32, name="y%d" % c, tag="bank%d" % c)
            in_pair = slice(CHUNK * (c % 2), CHUNK * (c % 2 + 1))
            product(y, w1q, w1s, xg[:, CHUNK * c : CHUNK * (c + 1)], xgs[c // 2][:, in_pair])
            ys.append(y)

        w2b = sb.tile([P, PACK * N], BF16, name="w2b", align_bytes=ALIGN)
        w2q = sb.tile([P, N], U32, name="w2q", align_bytes=ALIGN)
        w2s = sb.tile([P, N], U8, name="w2s", align_bytes=ALIGN)
        for h in range(2):
            nc.scalar.copy(
                w2b[:].rearrange("p (t m j) -> p m t j", t=PACK, j=PACK)[:, HALF_M * h : HALF_M * (h + 1)],
                dealt(w2_raw[h]),
            )

        def group_means(c):
            sums = sb.tile([P, GROUPS, PACK], F32, name="sums%d" % c)
            mean = sb.tile([P, GROUPS, PACK], F32, name="mean%d" % c)
            nc.vector.tensor_reduce(
                out=sums[:], in_=ys[c][:].rearrange("p t (v d) -> p v t d", d=D), axis=AXIS.X, op=ALU.add
            )
            nc.gpsimd.tensor_scalar(mean[:], sums[:], 1.0 / D, 0.0, ALU.mult, ALU.add)
            return mean

        def centre(c, mean):
            dd = sb.tile([P, GROUPS, D, PACK], F32, name="dd%d" % c, tag="dd%d" % c, align_bytes=ALIGN)
            nc.vector.tensor_tensor(
                dd[:],
                ys[c][:].rearrange("p t (v d) -> p v d t", d=D),
                mean[:].unsqueeze(2).to_broadcast([P, GROUPS, D, PACK]),
                ALU.subtract,
            )
            return dd

        ee = [
            sb.tile([P, HALF_D, 2 * STATS], F32, name="ee%d" % h, tag="w2_raw%d" % h, align_bytes=ALIGN)
            for h in range(2)
        ]
        dds = []
        means = [group_means(c) for c in (0, 1)]
        for c in (0, 1):
            dds.append(centre(c, means[c]))
            for h in range(2):
                nc.scalar.activation(
                    ee[h][:, :, STATS * c : STATS * (c + 1)].rearrange("p d (v t) -> p d v t", t=PACK),
                    dds[c][:].rearrange("p v d t -> p d v t")[:, HALF_D * h : HALF_D * (h + 1)],
                    ACT.Square,
                )
        turned = ps.tile([P, 2, P], F32, name="turned", tag="bank4")
        for d in range(D):
            nc.tensor.matmul(
                turned[:, 0, :],
                ee[d // HALF_D][:, d % HALF_D, :],
                ident[:],
                start=(d == 0),
                stop=(d == D - 1),
                is_transpose=True,
            )

        squares = []
        means = [group_means(c) for c in (2, 3)]
        for c in (2, 3):
            dds.append(centre(c, means[c - 2]))
            sq = sb.tile([P, 2 * GROUPS, PACK, HALF_D], F32, name="sq%d" % c)
            nc.scalar.activation(sq[:], dds[c][:].rearrange("p v (h i) t -> p (v h) t i", i=HALF_D), ACT.Square)
            squares.append(sq)

        nc.vector.quantize_mx(out=w2q[:].bitcast(FP8X4), scales=w2s[:], in_=w2b[:])

        def with_gain(name, tag, inv_dev, groups):
            factor = sb.tile([P, groups, PACK], F32, name=name, tag=tag, align_bytes=ALIGN)
            nc.vector.tensor_tensor(
                factor[:], inv_dev, gam_sb[:].unsqueeze(1).to_broadcast([P, groups, PACK]), ALU.mult
            )
            return factor

        factors = {}
        for c in (2, 3):
            ssq = sb.tile([P, GROUPS, PACK], F32, name="ssq%d" % c, tag="ssq%d" % c, align_bytes=ALIGN)
            inv_dev = sb.tile([P, GROUPS, PACK], F32, name="inv_dev%d" % c)
            nc.vector.tensor_reduce(
                out=ssq[:], in_=squares[c - 2][:].rearrange("p (v h) t i -> p v t h i", h=2), axis=AXIS.XY, op=ALU.add
            )
            nc.scalar.activation(inv_dev[:], ssq[:], ACT.Abs_reciprocal_sqrt, bias=eps, scale=1.0 / D)
            factors[c] = with_gain("factor%d" % c, "factor%d" % c, inv_dev[:], GROUPS)[:]

        inv_dev_turned = sb.tile([P, P], F32, name="inv_dev_turned", tag="ssq2", align_bytes=ALIGN)
        nc.scalar.activation(inv_dev_turned[:], turned[:, 0, :], ACT.Abs_reciprocal_sqrt, bias=eps, scale=1.0 / D)
        nc.tensor.transpose(turned[:, 1, :], inv_dev_turned[:], ident[:])

        outs = []

        def second_layer(i, z_tag):
            first, width = PIECES[i]
            c, v0, groups = first // CHUNK, (first % CHUNK) // D, width // D
            zb = sb.tile([P, groups, D, PACK], BF16, name="zb%d" % i, tag=z_tag, align_bytes=ALIGN)
            zq = sb.tile([P, width], U32, name="zq%d" % i, align_bytes=ALIGN)
            zs = sb.tile([P, width], U8, name="zs%d" % i, align_bytes=ALIGN)
            nc.vector.tensor_tensor(
                zb[:],
                dds[c][:, v0 : v0 + groups],
                factors[c][:, v0 : v0 + groups, :].unsqueeze(2).to_broadcast([P, groups, D, PACK]),
                ALU.mult,
            )
            nc.vector.quantize_mx(out=zq[:].bitcast(FP8X4), scales=zs[:], in_=zb[:].rearrange("p v d t -> p (v d t)"))
            acc = ps.tile([P, PACK, width], F32, name="acc%d" % i, tag="bank%d" % ((5 + i) % 8))
            product(acc, w2q, w2s, zq[:], zs[:])
            outs.append(acc)

        second_layer(0, "zb_first")
        second_layer(1, "zb_first")
        factor01 = with_gain("factor01", "dd2", turned[:, 1, :].rearrange("p (v t) -> p v t", t=PACK), 2 * GROUPS)
        factors[0], factors[1] = factor01[:, 0:GROUPS, :], factor01[:, GROUPS : 2 * GROUPS, :]
        for i in range(2, len(PIECES)):
            second_layer(i, "zb%d" % i)

        ob = sb.tile([P, S, PACK], BF16, name="ob", align_bytes=ALIGN)
        oq = sb.tile([P, S], U32, name="oq", align_bytes=ALIGN)
        osc = sb.tile([P, S], U8, name="osc", align_bytes=ALIGN)
        out_rows = out_0.rearrange("(p t) n -> p t n", t=PACK)
        out_words = out_1[0].rearrange("p n t -> p (n t)").bitcast(I32)
        last = len(PIECES) - 1

        def round_from_bank(copy, i):
            first, width = PIECES[i]
            copy(ob[:, first : first + width, :], outs[i][:].rearrange("p t n -> p n t"))

        def planes(first, end):
            nc.vector.quantize_mx(
                out=oq[:, first:end].bitcast(FP8X4),
                scales=osc[:, first:end],
                in_=ob[:, first:end, :].rearrange("p n t -> p (n t)"),
            )

        staged = []
        for i, (first, width) in enumerate(PIECES):
            if first % CHUNK == 0:
                o32 = sb.tile([P, PACK, CHUNK], F32, name="o32_%d" % i)
            part = o32[:, :, first % CHUNK : first % CHUNK + width]
            if i == last:
                round_from_bank(nc.vector.tensor_copy, i)
            nc.scalar.copy(part, outs[i][:])
            if (first + width) % CHUNK == 0:
                nc.sync.dma_start(out_rows[:, :, first + width - CHUNK : first + width], o32[:])
            staged.append(part)

        for i in (0, 1):
            round_from_bank(nc.scalar.copy, i)
        planes(PAIR, S)
        nc.sync.dma_start(out_words[:, PAIR:S], oq[:, PAIR:S].bitcast(I32))
        for i in (2, 3):
            first, width = PIECES[i]
            nc.vector.tensor_copy(
                ob[:, first : first + width, :].rearrange("p (a i) t -> p a t i", i=4),
                staged[i].rearrange("p t (a i) -> p a t i", i=4),
            )
            if i == 2:
                planes(0, CHUNK)
        planes(CHUNK, PAIR)
        nc.sync.dma_start(out_words[:, 0:PAIR], oq[:, 0:PAIR].bitcast(I32))
        for q in range(P // QUADRANT):
            queue = nc.sync if q % 2 == 0 else nc.scalar
            queue.dma_start(
                out_2[0, PACK * q : PACK * (q + 1), :].bitcast(I32),
                osc[QUADRANT * q : QUADRANT * q + PACK, :].bitcast(I32),
            )
